import numpy as np
import ml_dtypes


def mxq(x, axis, fmt="e4m3"):
    dtype, down = {"e4m3": (ml_dtypes.float8_e4m3fn, 7), "e5m2": (ml_dtypes.float8_e5m2, 14)}[fmt]
    v = np.moveaxis(np.asarray(x, np.float32).astype(ml_dtypes.bfloat16).astype(np.float64), axis, -1)
    blocks = v.reshape(v.shape[:-1] + (-1, 32))
    amax = np.abs(blocks).max(-1, keepdims=True)
    byte = np.maximum(np.where(amax > 0, np.frexp(amax)[1] - 1 + 127, 0) - down, 1)
    scale = np.exp2(byte - 127.0)
    codes = (blocks / scale).astype(np.float32).astype(dtype).astype(np.float64)
    return np.moveaxis((codes * scale).reshape(v.shape), -1, axis)


WIDE = False


def mx_kscale(k):
    if not WIDE:
        return np.ones(k)
    levels = np.array([10, -10, 5, -5, 0])
    if k % 512:
        return np.exp2(np.random.permutation(np.resize(levels, k // 32))).repeat(32)
    a = np.empty((k // 512, 16))
    for p in range(k // 512):
        a[p, :8] = np.random.permutation(np.resize(levels, 8))
        for g in range(8):
            far = levels[np.abs(levels - a[p, g]) >= 10]
            a[p, g + 8] = far[np.random.randint(len(far))]
    return np.exp2(a.ravel()).repeat(32)


def f64(x):
    return np.asarray(x).astype(np.float64)


def striped(idx):
    return np.tile(np.asarray(idx).reshape(-1, 16).T, (8, 1)).astype(np.uint16)


def unstriped(offs):
    return offs[:16].T.reshape(-1).astype(np.int64)


def striped8(idx):
    return np.asarray(idx).reshape(8, -1, 16).transpose(0, 2, 1).reshape(128, -1).astype(np.uint16)


def unstriped8(offs):
    return offs.reshape(8, 16, -1).transpose(0, 2, 1).reshape(8, -1).astype(np.int64)


def pick8(x, idx, run):
    r = np.arange(len(x))
    return x[r[:, None], idx[r % (8 * run) // run]]


E2M1 = np.array([0.0, 0.5, 1.0, 1.5, 2.0, 3.0, 4.0, 6.0, -0.0, -0.5, -1.0, -1.5, -2.0, -3.0, -4.0, -6.0])


def pack_weight(w, fmt):
    k, n = w.shape
    w = f64(np.asarray(w, np.float32).astype(ml_dtypes.bfloat16)).reshape(k // 32, 32, n)
    amax = np.abs(w).max(1)
    if fmt == "e4m3":
        byte = np.frexp(amax)[1] - 1 + 127 - 7
    else:
        mant, ex = np.frexp(amax / 6.0)
        byte = np.where(mant > 0.5, ex, ex - 1) + 127
    byte = np.clip(np.where(amax > 0, byte, 1), 1, 254)
    scaled = (w * np.exp2(127.0 - byte)[:, None, :]).reshape(k, n).astype(np.float32)
    by_word = np.ascontiguousarray(scaled.reshape(k // 512, 128, 4, n).transpose(0, 1, 3, 2))
    if fmt == "e4m3":
        words = by_word.astype(ml_dtypes.float8_e4m3fn).view(np.uint8)
    else:
        c = by_word.astype(ml_dtypes.float4_e2m1fn).view(np.uint8) & 0xF
        words = (c[..., 0::2] | (c[..., 1::2] << 4)).reshape(k // 512, 128, 2 * n)
    return np.ascontiguousarray(words), np.ascontiguousarray(byte.astype(np.uint8).reshape(k // 512, 16, n))


def unpack_weight(words, scales, fmt):
    g, _, n = scales.shape
    words = np.ascontiguousarray(words).reshape(g, 128, n, -1)
    if fmt == "e4m3":
        vals = words.view(ml_dtypes.float8_e4m3fn).astype(np.float64)
    else:
        nib = np.empty((g, 128, n, 4), np.uint8)
        nib[..., 0::2] = words & 0xF
        nib[..., 1::2] = words >> 4
        vals = E2M1[nib]
    vals = vals * np.repeat(np.exp2(scales.astype(np.float64) - 127.0), 8, axis=1)[..., None]
    return vals.transpose(0, 1, 3, 2).reshape(g * 512, n)


K, R, F, T, J, M = 512, 128, 512, 2048, 512, 256


def setup_inputs():
    n = np.random.standard_normal
    idx = np.random.permutation(T)[:J]
    idx2 = np.stack([np.random.permutation(J)[:M] for _ in range(8)])
    idx3 = np.stack([np.random.permutation(J)[:M] for _ in range(8)])
    fk = mx_kscale(K)
    ff = mx_kscale(F)
    fj = mx_kscale(J)
    tj = np.ones(T)
    tj[idx] = fj
    tabp = pack_weight(n((K, T)) / fk[:, None], "e4m3")
    return {
        "tab_words": tabp[0],
        "tab_scales": tabp[1],
        "w1": (n((K, R)) * 1 / np.sqrt(K) * fk[:, None]).astype(np.float32),
        "sharp": (np.random.uniform(0.1, 0.5, (1, M))).astype(np.float32),
        "wo": (n((F, R)) * 1 / np.sqrt(F) * ff[:, None]).astype(np.float32),
        "dy": (n((F, M)) / ff[:, None]).astype(np.float32),
        "js": (np.random.uniform(0.5, 2.0, (1, J)) * fj).astype(np.float32),
        "xrows": (n((K, T)) / tj).astype(np.float32),
        "old": (n((K, R)) * 4.0).astype(np.float32),
        "offs": striped(idx),
        "offs2": striped8(idx2),
        "offs3": striped8(idx3),
    }


def reference(tab_words, tab_scales, w1, sharp, wo, dy, js, xrows, old, offs, offs2, offs3):
    idx = unstriped(offs)
    idx2 = unstriped8(offs2)
    idx3 = unstriped8(offs3)
    tabu = unpack_weight(tab_words, tab_scales, "e4m3")
    w1q = mxq(f64(w1), 0, "e4m3")
    tabidxg = tabu[:, idx]
    a = w1q.T @ tabidxg
    dl = pick8(a, idx2, 16) - pick8(a, idx3, 16)
    u1 = np.exp(np.square(dl) * f64(sharp) * (-1.0))
    woq = mxq(f64(wo), 0, "e4m3")
    dyq = mxq(f64(dy), 0, "e4m3")
    c0 = woq.T @ dyq
    ddl = c0 * u1 * (-1.0) * f64(sharp) * dl * 2.0
    s1 = np.zeros((R, J))
    s1[np.arange(R)[:, None], idx2[np.arange(R) % 128 // 16]] = ddl
    e2 = ddl * (-1.0)
    s2 = np.zeros((R, J))
    s2[np.arange(R)[:, None], idx3[np.arange(R) % 128 // 16]] = e2
    da = s1 + s2
    gs = da * f64(js)
    gt1 = gs.T
    xt = f64(xrows)[:, idx].T
    xtq = mxq(xt, 0, "e4m3")
    gt1q = mxq(gt1, 0, "e4m3")
    gw = xtq.T @ gt1q
    y = gw + f64(old)
    return y

@@ -1,0 +1,179 @@
+from contextlib import ExitStack
+
+import concourse.mybir as mybir
+from concourse.masks import make_identity
+
+K, R, F, T, J, M = 512, 128, 512, 2048, 512, 256
+P = 128
+FLOPS = 2 * (K * R * J + F * R * M + J * K * R)
+
+F32 = mybir.dt.float32
+BF16 = mybir.dt.bfloat16
+I32 = mybir.dt.int32
+U32 = mybir.dt.uint32
+U16 = mybir.dt.uint16
+U8 = mybir.dt.uint8
+FP8X4 = mybir.dt.float8_e4m3fn_x4
+ALU = mybir.AluOpType
+ACT = mybir.ActivationFunctionType
+
+
+def tile_attend_cpairnear_w_kernel(tc, tab_words, tab_scales, w1, sharp, wo, dy, js, xrows, old, offs, offs2, offs3, out):
+    nc = tc.nc
+    with ExitStack() as ctx:
+        lists = ctx.enter_context(tc.tile_pool(name="lists", bufs=1))
+        sb = ctx.enter_context(tc.tile_pool(name="sb", bufs=1))
+        ps = ctx.enter_context(tc.psum_pool(name="ps", bufs=1))
+
+        def tile(shape, dtype, name):
+            return sb.tile(shape, dtype, name=name, align_bytes=64)
+
+        def quantize(grouped, words, name, reuse=None):
+            codes = tile([P, words], U32, reuse or name + "_codes")
+            scales = tile([P, words], U8, name + "_scales")
+            nc.vector.quantize_mx(out=codes[:].bitcast(FP8X4), scales=scales[:], in_=grouped)
+            return codes, scales
+
+        def product(acc, lhs, rhs):
+            nc.tensor.matmul_mx(out=acc, lhsT=lhs[0].bitcast(FP8X4), lhsT_scale=lhs[1],
+                                rhs=rhs[0].bitcast(FP8X4), rhs_scale=rhs[1], start=True, stop=True)
+
+        idx = lists.tile([P, J // 16], U16, name="idx")
+        idx2 = lists.tile([P, M // 16], U16, name="idx2")
+        idx3 = lists.tile([P, M // 16], U16, name="idx3")
+        tab_b = tile([P, T], U8, "tab_b")
+        tab_w = tile([P, T], U32, "tab_w")
+        nc.vector.memset(tab_b[:].bitcast(I32), 0)
+        stage_b = tile([P, T // 4], I32, "stage_b")
+        nc.sync.dma_start(idx[:], offs)
+        for q in range(4):
+            nc.scalar.dma_start(stage_b[32 * q : 32 * q + 4, :], tab_scales[0, 4 * q : 4 * q + 4, :].bitcast(I32))
+        w1_raw = tile([P, 4, R], F32, "w1_raw")
+        nc.sync.dma_start(w1_raw[:], w1.rearrange("(p t) r -> p t r", t=4))
+        nc.sync.dma_start(tab_w[:].bitcast(I32), tab_words[0].rearrange("p n t -> p (n t)").bitcast(I32))
+        wo_raw = tile([P, 4, R], F32, "wo_raw")
+        nc.sync.dma_start(wo_raw[:], wo.rearrange("(p t) r -> p t r", t=4))
+        nc.sync.dma_start(idx2[:], offs2)
+        nc.sync.dma_start(idx3[:], offs3)
+        sharp_col = tile([P, 2], F32, "sharp_col")
+        nc.sync.dma_start(sharp_col[:], sharp.rearrange("o (p e) -> p (o e)", e=2))
+        dy_raw = tile([P, 4, M], F32, "dy_raw")
+        nc.sync.dma_start(dy_raw[:], dy.rearrange("(p t) m -> p t m", t=4))
+        x_rows = xrows.rearrange("(p g) t -> g p t", g=4)
+        x_raw = [tile([P, T], F32, "x_raw%d" % g) for g in range(4)]
+        js_col = tile([P, 4], F32, "js_col")
+        old_sb = tile([P, 4, R], F32, "old_sb")
+        for g in range(4):
+            if g == 2:
+                nc.sync.dma_start(js_col[:], js.rearrange("o (p t) -> p (o t)", t=4))
+            nc.sync.dma_start(x_raw[g][:], x_rows[g])
+        nc.sync.dma_start(old_sb[:], old.rearrange("(p g) r -> p g r", g=4))
+
+        ident = tile([P, P], F32, "ident")
+        make_identity(nc, ident[:])
+        s1 = tile([P, J], F32, "s1")
+        s2 = tile([P, J], F32, "s2")
+        nc.vector.memset(s1[:], 0.0)
+        nc.vector.memset(s2[:], 0.0)
+        warm = tile([P, 1], F32, "warm")
+        nc.scalar.activation(warm[:], s2[:, 0:1], ACT.Exp)
+
+        for q in range(4):
+            nc.vector.tensor_copy(tab_b[32 * q : 32 * q + 4, :].bitcast(I32), stage_b[32 * q : 32 * q + 4, :])
+        w1_bf = tile([P, R, 4], BF16, "w1_bf")
+        nc.scalar.copy(w1_bf[:], w1_raw[:].rearrange("p t r -> p r t"))
+        w1_q = quantize(w1_bf[:].rearrange("p r t -> p (r t)"), R, "w1")
+        g_b = tile([P, J], U8, "g_b")
+        nc.vector.tensor_copy(g_b[:], tab_b[:].indirect(idx[:]))
+        g_w = tile([P, J], U32, "g_w")
+        a = tile([P, J], F32, "a")
+        half = J // 2
+        for h in range(2):
+            cols = slice(h * half, (h + 1) * half)
+            nc.vector.tensor_copy(g_w[:, cols], tab_w[:].indirect(idx[:, h * half // 16 : (h + 1) * half // 16]))
+        a_ps = [ps.tile([P, half], F32, name="a_ps%d" % h) for h in range(2)]
+        for h in range(2):
+            cols = slice(h * half, (h + 1) * half)
+            product(a_ps[h][:], (w1_q[0][:], w1_q[1][:]), (g_w[:, cols], g_b[:, cols]))
+        wo_bf = tile([P, R, 4], BF16, "wo_bf")
+        nc.scalar.copy(wo_bf[:], wo_raw[:].rearrange("p t r -> p r t"))
+        dy_bf = tile([P, M, 4], BF16, "dy_bf")
+        nc.scalar.copy(dy_bf[:], dy_raw[:].rearrange("p t m -> p m t"))
+        nc.vector.tensor_copy(a[:, 0:half], a_ps[0][:])
+        wo_q = quantize(wo_bf[:].rearrange("p r t -> p (r t)"), R, "wo", "tab_b")
+        nc.vector.tensor_copy(a[:, half:J], a_ps[1][:])
+
+        sharp_ps = ps.tile([P, 2, P], F32, name="a_ps0")
+        for e in range(2):
+            nc.tensor.transpose(sharp_ps[:, e, :], sharp_col[:, e : e + 1].to_broadcast([P, P]), ident[:])
+
+        def gather_x(x_g, g, lo, hi):
+            nc.vector.tensor_copy(x_g[:, lo:hi], x_raw[g][:].indirect(idx[:, lo // 16 : hi // 16]))
+
+        def turn_x(x_g, g):
+            words = x_g[:].bitcast(F32)
+            xt_ps = ps.tile([P, 2, P], F32, name="xt_ps%d" % (g % 2))
+            for u in range(2):
+                nc.tensor.transpose(xt_ps[:, u, :], words[:, u : J // 2 : 2], ident[:])
+            xt_bf = tile([P, 4 * P], BF16, "xt_bf%d" % g)
+            nc.scalar.copy(xt_bf[:].bitcast(F32).rearrange("p (k u) -> p k u", u=2), xt_ps[:].rearrange("p u k -> p k u"))
+            return xt_bf
+
+        a3 = tile([P, M], F32, "a3")
+        nc.vector.tensor_copy(a3[:], a[:].indirect(idx3[:]))
+        dy_q = quantize(dy_bf[:].rearrange("p m t -> p (m t)"), M, "dy", "g_w")
+        c0_ps = ps.tile([P, M], F32, name="c0_ps")
+        product(c0_ps[:], (wo_q[0][:], wo_q[1][:]), (dy_q[0][:], dy_q[1][:]))
+        dl = tile([P, M], F32, "dl")
+        nc.vector.tensor_tensor(dl[:], a[:].indirect(idx2[:]), a3[:], ALU.subtract)
+        x_g = [tile([P, J], BF16, "dy_bf")]
+        gather_x(x_g[0], 0, 0, 128)
+        ds = tile([P, M], F32, "ds")
+        nc.vector.tensor_tensor(ds[:].rearrange("p (n e) -> p n e", e=2), dl[:].rearrange("p (n e) -> p n e", e=2),
+                                sharp_ps[:].rearrange("p e n -> p n e"), ALU.mult)
+        gather_x(x_g[0], 0, 128, 256)
+        sq = tile([P, M], F32, "sq")
+        nc.vector.tensor_tensor(sq[:], ds[:], dl[:], ALU.mult)
+        u1 = tile([P, M], F32, "u1")
+        nc.scalar.activation(u1[:], sq[:], ACT.Exp, scale=-1.0)
+        coef = tile([P, M], F32, "coef")
+        nc.vector.scalar_tensor_tensor(coef[:], ds[:], -2.0, c0_ps[:], ALU.mult, ALU.mult)
+        ncoef = tile([P, M], F32, "ncoef")
+        nc.scalar.activation(ncoef[:], coef[:], ACT.Copy, scale=-1.0)
+        gather_x(x_g[0], 0, 256, 512)
+        nc.vector.tensor_tensor(s1[:].indirect(idx2[:]), coef[:], u1[:], ALU.mult)
+        nc.vector.tensor_tensor(s2[:].indirect(idx3[:]), ncoef[:], u1[:], ALU.mult)
+        xt = [turn_x(x_g[0], 0)]
+
+        da_ps = ps.tile([P, 4, R], F32, name="da_ps")
+        for i, s in enumerate((s1, s2)):
+            for t in range(4):
+                nc.tensor.matmul(da_ps[:, t, :], s[:, t:J:4], ident[:], is_transpose=True,
+                                 start=(i == 0 and t == 0), stop=(i == 1 and t == 3))
+
+        x_g.append(tile([P, J], BF16, "coef"))
+        gather_x(x_g[1], 1, 0, J)
+        xt.append(turn_x(x_g[1], 1))
+        gt_bf = tile([P, R, 4], BF16, "gt_bf")
+        nc.vector.tensor_tensor(gt_bf[:], da_ps[:].rearrange("p t r -> p r t"),
+                                js_col[:].unsqueeze(1).to_broadcast([P, R, 4]), ALU.mult)
+        x_g.append(tile([P, J], BF16, "ncoef"))
+        gather_x(x_g[2], 2, 0, J)
+        xt.append(turn_x(x_g[2], 2))
+        gt_q = quantize(gt_bf[:].rearrange("p r t -> p (r t)"), R, "gt")
+        x_g.append(tile([P, J], BF16, "js_col"))
+        gather_x(x_g[3], 3, 0, J)
+        xt.append(turn_x(x_g[3], 3))
+        xt_q = [quantize(xt[g][:], P, "xt%d" % g) for g in range(3)]
+        res = tile([P, 4, R], F32, "res")
+        out_rows = out.rearrange("(p g) r -> p g r", g=4)
+        gw_a = ps.tile([P, 3, R], F32, name="gw_a")
+        for g in range(3):
+            product(gw_a[:, g, :], (xt_q[g][0][:], xt_q[g][1][:]), (gt_q[0][:], gt_q[1][:]))
+        nc.vector.tensor_tensor(res[:, 0:3, :], gw_a[:], old_sb[:, 0:3, :], ALU.add)
+        nc.sync.dma_start(out_rows[:, 0:3, :], res[:, 0:3, :])
+        xt_q.append(quantize(xt[3][:], P, "xt3"))
+        gw_b = ps.tile([P, half], F32, name="a_ps1")
+        product(gw_b[:, 0:R], (xt_q[3][0][:], xt_q[3][1][:]), (gt_q[0][:], gt_q[1][:]))
+        nc.vector.tensor_tensor(res[:, 3, :], gw_b[:, 0:R], old_sb[:, 3, :], ALU.add)
+        nc.sync.dma_start(out_rows[:, 3, :], res[:, 3, :])

@@ -47,9 +47,9 @@ def tile_attend_cpairnear_w_kernel(tc, tab_words, tab_scales, w1, sharp, wo, dy,
         stage_b = tile([P, T // 4], I32, "stage_b")
         nc.sync.dma_start(idx[:], offs)
         for q in range(4):
-            nc.scalar.dma_start(stage_b[32 * q : 32 * q + 4, :], tab_scales[0, 4 * q : 4 * q + 4, :].bitcast(I32))
+            (nc.sync, nc.scalar)[q % 2].dma_start(stage_b[32 * q : 32 * q + 4, :], tab_scales[0, 4 * q : 4 * q + 4, :].bitcast(I32))
         w1_raw = tile([P, 4, R], F32, "w1_raw")
-        nc.sync.dma_start(w1_raw[:], w1.rearrange("(p t) r -> p t r", t=4))
+        nc.scalar.dma_start(w1_raw[:], w1.rearrange("(p t) r -> p t r", t=4))
         nc.sync.dma_start(tab_w[:].bitcast(I32), tab_words[0].rearrange("p n t -> p (n t)").bitcast(I32))
         wo_raw = tile([P, 4, R], F32, "wo_raw")
         nc.sync.dma_start(wo_raw[:], wo.rearrange("(p t) r -> p t r", t=4))
@@ -60,10 +60,13 @@ def tile_attend_cpairnear_w_kernel(tc, tab_words, tab_scales, w1, sharp, wo, dy,
         dy_raw = tile([P, 4, M], F32, "dy_raw")
         nc.sync.dma_start(dy_raw[:], dy.rearrange("(p t) m -> p t m", t=4))
         x_rows = xrows.rearrange("(p g) t -> g p t", g=4)
-        x_raw = [tile([P, T], F32, "x_raw%d" % g) for g in range(4)]
+        x0_halves = [tile([P, T // 2], F32, "x0_half%d" % h) for h in range(2)]
+        x_raw = [None] + [tile([P, T], F32, "x_raw%d" % g) for g in range(1, 4)]
+        for h in range(2):
+            nc.sync.dma_start(x0_halves[h][:], x_rows[0][:, h * T // 2 : (h + 1) * T // 2])
         js_col = tile([P, 4], F32, "js_col")
         old_sb = tile([P, 4, R], F32, "old_sb")
-        for g in range(4):
+        for g in range(1, 4):
             if g == 2:
                 nc.sync.dma_start(js_col[:], js.rearrange("o (p t) -> p (o t)", t=4))
             nc.sync.dma_start(x_raw[g][:], x_rows[g])
@@ -100,50 +103,51 @@ def tile_attend_cpairnear_w_kernel(tc, tab_words, tab_scales, w1, sharp, wo, dy,
         dy_bf = tile([P, M, 4], BF16, "dy_bf")
         nc.scalar.copy(dy_bf[:], dy_raw[:].rearrange("p t m -> p m t"))
         nc.vector.tensor_copy(a[:, 0:half], a_ps[0][:])
-        wo_q = quantize(wo_bf[:].rearrange("p r t -> p (r t)"), R, "wo", "tab_b")
         nc.vector.tensor_copy(a[:, half:J], a_ps[1][:])
+        wo_q = quantize(wo_bf[:].rearrange("p r t -> p (r t)"), R, "wo", "tab_w")
 
         sharp_ps = ps.tile([P, 2, P], F32, name="a_ps0")
         for e in range(2):
             nc.tensor.transpose(sharp_ps[:, e, :], sharp_col[:, e : e + 1].to_broadcast([P, P]), ident[:])
 
-        def gather_x(x_g, g, lo, hi):
-            nc.vector.tensor_copy(x_g[:, lo:hi], x_raw[g][:].indirect(idx[:, lo // 16 : hi // 16]))
-
-        def turn_x(x_g, g):
+        def turn_x(x_g, xt_words, bank):
             words = x_g[:].bitcast(F32)
-            xt_ps = ps.tile([P, 2, P], F32, name="xt_ps%d" % (g % 2))
+            xt_ps = ps.tile([P, 2, P], F32, name=bank)
             for u in range(2):
                 nc.tensor.transpose(xt_ps[:, u, :], words[:, u : J // 2 : 2], ident[:])
-            xt_bf = tile([P, 4 * P], BF16, "xt_bf%d" % g)
-            nc.scalar.copy(xt_bf[:].bitcast(F32).rearrange("p (k u) -> p k u", u=2), xt_ps[:].rearrange("p u k -> p k u"))
-            return xt_bf
+            nc.scalar.copy(xt_words.rearrange("p (k u) -> p k u", u=2), xt_ps[:].rearrange("p u k -> p k u"))
 
+        x0_bf = tile([P, T], BF16, "x0_bf")
+        for h in range(2):
+            nc.scalar.copy(x0_bf[:, h * T // 2 : (h + 1) * T // 2], x0_halves[h][:])
+        parts = [slice(0, M // 2), slice(M // 2, M)]
+        offsets = [slice(0, M // 32), slice(M // 32, M // 16)]
         a3 = tile([P, M], F32, "a3")
-        nc.vector.tensor_copy(a3[:], a[:].indirect(idx3[:]))
-        dy_q = quantize(dy_bf[:].rearrange("p m t -> p (m t)"), M, "dy", "g_w")
+        ds = tile([P, M], F32, "ds")
+        sq = tile([P, M], F32, "sq")
+        u1 = tile([P, M], F32, "x0_half1")
+        coef = tile([P, M], F32, "coef")
+        nu1 = tile([P, M], F32, "nu1")
+        for h in range(2):
+            nc.vector.tensor_copy(a3[:, parts[h]], a[:].indirect(idx3[:, offsets[h]]))
+        dy_q = quantize(dy_bf[:].rearrange("p m t -> p (m t)"), M, "dy")
         c0_ps = ps.tile([P, M], F32, name="c0_ps")
         product(c0_ps[:], (wo_q[0][:], wo_q[1][:]), (dy_q[0][:], dy_q[1][:]))
-        dl = tile([P, M], F32, "dl")
-        nc.vector.tensor_tensor(dl[:], a[:].indirect(idx2[:]), a3[:], ALU.subtract)
-        x_g = [tile([P, J], BF16, "dy_bf")]
-        gather_x(x_g[0], 0, 0, 128)
-        ds = tile([P, M], F32, "ds")
-        nc.vector.tensor_tensor(ds[:].rearrange("p (n e) -> p n e", e=2), dl[:].rearrange("p (n e) -> p n e", e=2),
-                                sharp_ps[:].rearrange("p e n -> p n e"), ALU.mult)
-        gather_x(x_g[0], 0, 128, 256)
-        sq = tile([P, M], F32, "sq")
-        nc.vector.tensor_tensor(sq[:], ds[:], dl[:], ALU.mult)
-        u1 = tile([P, M], F32, "u1")
-        nc.scalar.activation(u1[:], sq[:], ACT.Exp, scale=-1.0)
-        coef = tile([P, M], F32, "coef")
+        dl = tile([P, M], F32, "dy_bf")
+        for h in range(2):
+            nc.vector.tensor_tensor(dl[:, parts[h]], a[:].indirect(idx2[:, offsets[h]]), a3[:, parts[h]], ALU.subtract)
+        for h in range(2):
+            nc.vector.tensor_tensor(ds[:, parts[h]].rearrange("p (n e) -> p n e", e=2), dl[:, parts[h]].rearrange("p (n e) -> p n e", e=2),
+                                    sharp_ps[:, :, 64 * h : 64 * h + 64].rearrange("p e n -> p n e"), ALU.mult)
+        for h in range(2):
+            nc.vector.tensor_tensor(sq[:, parts[h]], ds[:, parts[h]], dl[:, parts[h]], ALU.mult)
+            nc.scalar.activation(u1[:, parts[h]], sq[:, parts[h]], ACT.Exp, scale=-1.0)
+        for h in range(2):
+            nc.scalar.activation(nu1[:, parts[h]], u1[:, parts[h]], ACT.Copy, scale=-1.0)
         nc.vector.scalar_tensor_tensor(coef[:], ds[:], -2.0, c0_ps[:], ALU.mult, ALU.mult)
-        ncoef = tile([P, M], F32, "ncoef")
-        nc.scalar.activation(ncoef[:], coef[:], ACT.Copy, scale=-1.0)
-        gather_x(x_g[0], 0, 256, 512)
-        nc.vector.tensor_tensor(s1[:].indirect(idx2[:]), coef[:], u1[:], ALU.mult)
-        nc.vector.tensor_tensor(s2[:].indirect(idx3[:]), ncoef[:], u1[:], ALU.mult)
-        xt = [turn_x(x_g[0], 0)]
+        for h in range(2):
+            nc.vector.tensor_tensor(s1[:].indirect(idx2[:, offsets[h]]), coef[:, parts[h]], u1[:, parts[h]], ALU.mult)
+            nc.vector.tensor_tensor(s2[:].indirect(idx3[:, offsets[h]]), coef[:, parts[h]], nu1[:, parts[h]], ALU.mult)
 
         da_ps = ps.tile([P, 4, R], F32, name="da_ps")
         for i, s in enumerate((s1, s2)):
@@ -151,29 +155,40 @@ def tile_attend_cpairnear_w_kernel(tc, tab_words, tab_scales, w1, sharp, wo, dy,
                 nc.tensor.matmul(da_ps[:, t, :], s[:, t:J:4], ident[:], is_transpose=True,
                                  start=(i == 0 and t == 0), stop=(i == 1 and t == 3))
 
-        x_g.append(tile([P, J], BF16, "coef"))
-        gather_x(x_g[1], 1, 0, J)
-        xt.append(turn_x(x_g[1], 1))
-        gt_bf = tile([P, R, 4], BF16, "gt_bf")
+        xt01 = tile([P, 2 * J], BF16, "xt01")
+        xt2 = tile([P, J], BF16, "xt2")
+        xt3 = tile([P, J], BF16, "xt3")
+        x_g = [tile([P, J], BF16, "x_g0"), tile([P, J], BF16, "x_g1")]
+        nc.scalar.activation(x_g[0][:], x0_bf[:].indirect(idx[:]), ACT.Copy)
+        turn_x(x_g[0], xt01[:].bitcast(F32)[:, 0 : J // 2], "xt_ps0")
+        x1_bf = tile([P, T], BF16, "sq")
+        for c in range(0, T, T // 2):
+            nc.scalar.copy(x1_bf[:, c : c + T // 2], x_raw[1][:, c : c + T // 2])
+        nc.scalar.activation(x_g[1][:], x1_bf[:].indirect(idx[:]), ACT.Copy)
+        turn_x(x_g[1], xt01[:].bitcast(F32)[:, J // 2 : J], "xt_ps1")
+        x_g.append(tile([P, J], BF16, "x0_half1"))
+        nc.vector.tensor_copy(x_g[2][:], x_raw[2][:].indirect(idx[:]))
+        turn_x(x_g[2], xt2[:].bitcast(F32), "xt_ps0")
+        gt_bf = tile([P, R, 4], BF16, "x_raw2")
         nc.vector.tensor_tensor(gt_bf[:], da_ps[:].rearrange("p t r -> p r t"),
                                 js_col[:].unsqueeze(1).to_broadcast([P, R, 4]), ALU.mult)
-        x_g.append(tile([P, J], BF16, "ncoef"))
-        gather_x(x_g[2], 2, 0, J)
-        xt.append(turn_x(x_g[2], 2))
-        gt_q = quantize(gt_bf[:].rearrange("p r t -> p (r t)"), R, "gt")
-        x_g.append(tile([P, J], BF16, "js_col"))
-        gather_x(x_g[3], 3, 0, J)
-        xt.append(turn_x(x_g[3], 3))
-        xt_q = [quantize(xt[g][:], P, "xt%d" % g) for g in range(3)]
+        x_g.append(tile([P, J], BF16, "nu1"))
+        nc.vector.tensor_copy(x_g[3][:], x_raw[3][:].indirect(idx[:]))
+        turn_x(x_g[3], xt3[:].bitcast(F32), "c0_ps")
+        gt_q = quantize(gt_bf[:].rearrange("p r t -> p (r t)"), R, "gt", "x_raw3")
+        xq01 = quantize(xt01[:], 2 * P, "xq01", "x_raw2")
+        xq2 = quantize(xt2[:], P, "xq2", "xt01")
+        xq3 = quantize(xt3[:], P, "xq3")
         res = tile([P, 4, R], F32, "res")
         out_rows = out.rearrange("(p g) r -> p g r", g=4)
         gw_a = ps.tile([P, 3, R], F32, name="gw_a")
-        for g in range(3):
-            product(gw_a[:, g, :], (xt_q[g][0][:], xt_q[g][1][:]), (gt_q[0][:], gt_q[1][:]))
+        gt_op = (gt_q[0][:], gt_q[1][:])
+        for g in range(2):
+            product(gw_a[:, g, :], (xq01[0][:, g * P : (g + 1) * P], xq01[1][:, g * P : (g + 1) * P]), gt_op)
+        product(gw_a[:, 2, :], (xq2[0][:], xq2[1][:]), gt_op)
+        gw_b = ps.tile([P, half], F32, name="a_ps1")
+        product(gw_b[:, 0:R], (xq3[0][:], xq3[1][:]), gt_op)
         nc.vector.tensor_tensor(res[:, 0:3, :], gw_a[:], old_sb[:, 0:3, :], ALU.add)
         nc.sync.dma_start(out_rows[:, 0:3, :], res[:, 0:3, :])
-        xt_q.append(quantize(xt[3][:], P, "xt3"))
-        gw_b = ps.tile([P, half], F32, name="a_ps1")
-        product(gw_b[:, 0:R], (xt_q[3][0][:], xt_q[3][1][:]), (gt_q[0][:], gt_q[1][:]))
         nc.vector.tensor_tensor(res[:, 3, :], gw_b[:, 0:R], old_sb[:, 3, :], ALU.add)
-        nc.sync.dma_start(out_rows[:, 3, :], res[:, 3, :])
+        nc.scalar.dma_start(out_rows[:, 3, :], res[:, 3, :])

@@ -34,6 +34,9 @@ def tile_attend_cpairnear_w_kernel(tc, tab_words, tab_scales, w1, sharp, wo, dy,
             nc.vector.quantize_mx(out=codes[:].bitcast(FP8X4), scales=scales[:], in_=grouped)
             return codes, scales
 
+        def interleave(grouped, raw):
+            nc.scalar.activation(grouped[:].rearrange("p (c i) t -> p c t i", i=4), raw[:].rearrange("p t (c i) -> p c t i", i=4), ACT.Copy)
+
         def product(acc, lhs, rhs):
             nc.tensor.matmul_mx(out=acc, lhsT=lhs[0].bitcast(FP8X4), lhsT_scale=lhs[1],
                                 rhs=rhs[0].bitcast(FP8X4), rhs_scale=rhs[1], start=True, stop=True)
@@ -45,9 +48,9 @@ def tile_attend_cpairnear_w_kernel(tc, tab_words, tab_scales, w1, sharp, wo, dy,
         tab_w = tile([P, T], U32, "tab_w")
         nc.vector.memset(tab_b[:].bitcast(I32), 0)
         stage_b = tile([P, T // 4], I32, "stage_b")
-        nc.sync.dma_start(idx[:], offs)
         for q in range(4):
             (nc.sync, nc.scalar)[q % 2].dma_start(stage_b[32 * q : 32 * q + 4, :], tab_scales[0, 4 * q : 4 * q + 4, :].bitcast(I32))
+        nc.sync.dma_start(idx[:], offs)
         w1_raw = tile([P, 4, R], F32, "w1_raw")
         nc.scalar.dma_start(w1_raw[:], w1.rearrange("(p t) r -> p t r", t=4))
         nc.sync.dma_start(tab_w[:].bitcast(I32), tab_words[0].rearrange("p n t -> p (n t)").bitcast(I32))
@@ -78,13 +81,11 @@ def tile_attend_cpairnear_w_kernel(tc, tab_words, tab_scales, w1, sharp, wo, dy,
         s2 = tile([P, J], F32, "s2")
         nc.vector.memset(s1[:], 0.0)
         nc.vector.memset(s2[:], 0.0)
-        warm = tile([P, 1], F32, "warm")
-        nc.scalar.activation(warm[:], s2[:, 0:1], ACT.Exp)
 
         for q in range(4):
             nc.vector.tensor_copy(tab_b[32 * q : 32 * q + 4, :].bitcast(I32), stage_b[32 * q : 32 * q + 4, :])
         w1_bf = tile([P, R, 4], BF16, "w1_bf")
-        nc.scalar.copy(w1_bf[:], w1_raw[:].rearrange("p t r -> p r t"))
+        interleave(w1_bf, w1_raw)
         w1_q = quantize(w1_bf[:].rearrange("p r t -> p (r t)"), R, "w1")
         g_b = tile([P, J], U8, "g_b")
         nc.vector.tensor_copy(g_b[:], tab_b[:].indirect(idx[:]))
@@ -99,9 +100,9 @@ def tile_attend_cpairnear_w_kernel(tc, tab_words, tab_scales, w1, sharp, wo, dy,
             cols = slice(h * half, (h + 1) * half)
             product(a_ps[h][:], (w1_q[0][:], w1_q[1][:]), (g_w[:, cols], g_b[:, cols]))
         wo_bf = tile([P, R, 4], BF16, "wo_bf")
-        nc.scalar.copy(wo_bf[:], wo_raw[:].rearrange("p t r -> p r t"))
+        interleave(wo_bf, wo_raw)
         dy_bf = tile([P, M, 4], BF16, "dy_bf")
-        nc.scalar.copy(dy_bf[:], dy_raw[:].rearrange("p t m -> p m t"))
+        interleave(dy_bf, dy_raw)
         nc.vector.tensor_copy(a[:, 0:half], a_ps[0][:])
         nc.vector.tensor_copy(a[:, half:J], a_ps[1][:])
         wo_q = quantize(wo_bf[:].rearrange("p r t -> p (r t)"), R, "wo", "tab_w")
@@ -122,7 +123,7 @@ def tile_attend_cpairnear_w_kernel(tc, tab_words, tab_scales, w1, sharp, wo, dy,
             nc.scalar.copy(x0_bf[:, h * T // 2 : (h + 1) * T // 2], x0_halves[h][:])
         parts = [slice(0, M // 2), slice(M // 2, M)]
         offsets = [slice(0, M // 32), slice(M // 32, M // 16)]
-        a3 = tile([P, M], F32, "a3")
+        a3 = tile([P, M], F32, "wo_raw")
         ds = tile([P, M], F32, "ds")
         sq = tile([P, M], F32, "sq")
         u1 = tile([P, M], F32, "x0_half1")
@@ -133,7 +134,7 @@ def tile_attend_cpairnear_w_kernel(tc, tab_words, tab_scales, w1, sharp, wo, dy,
         dy_q = quantize(dy_bf[:].rearrange("p m t -> p (m t)"), M, "dy")
         c0_ps = ps.tile([P, M], F32, name="c0_ps")
         product(c0_ps[:], (wo_q[0][:], wo_q[1][:]), (dy_q[0][:], dy_q[1][:]))
-        dl = tile([P, M], F32, "dy_bf")
+        dl = tile([P, M], F32, "dy_raw")
         for h in range(2):
             nc.vector.tensor_tensor(dl[:, parts[h]], a[:].indirect(idx2[:, offsets[h]]), a3[:, parts[h]], ALU.subtract)
         for h in range(2):
@@ -142,9 +143,9 @@ def tile_attend_cpairnear_w_kernel(tc, tab_words, tab_scales, w1, sharp, wo, dy,
         for h in range(2):
             nc.vector.tensor_tensor(sq[:, parts[h]], ds[:, parts[h]], dl[:, parts[h]], ALU.mult)
             nc.scalar.activation(u1[:, parts[h]], sq[:, parts[h]], ACT.Exp, scale=-1.0)
+            nc.vector.scalar_tensor_tensor(coef[:, parts[h]], ds[:, parts[h]], -2.0, c0_ps[:, parts[h]], ALU.mult, ALU.mult)
         for h in range(2):
             nc.scalar.activation(nu1[:, parts[h]], u1[:, parts[h]], ACT.Copy, scale=-1.0)
-        nc.vector.scalar_tensor_tensor(coef[:], ds[:], -2.0, c0_ps[:], ALU.mult, ALU.mult)
         for h in range(2):
             nc.vector.tensor_tensor(s1[:].indirect(idx2[:, offsets[h]]), coef[:, parts[h]], u1[:, parts[h]], ALU.mult)
             nc.vector.tensor_tensor(s2[:].indirect(idx3[:, offsets[h]]), coef[:, parts[h]], nu1[:, parts[h]], ALU.mult)
@@ -155,40 +156,32 @@ def tile_attend_cpairnear_w_kernel(tc, tab_words, tab_scales, w1, sharp, wo, dy,
                 nc.tensor.matmul(da_ps[:, t, :], s[:, t:J:4], ident[:], is_transpose=True,
                                  start=(i == 0 and t == 0), stop=(i == 1 and t == 3))
 
-        xt01 = tile([P, 2 * J], BF16, "xt01")
-        xt2 = tile([P, J], BF16, "xt2")
-        xt3 = tile([P, J], BF16, "xt3")
         x_g = [tile([P, J], BF16, "x_g0"), tile([P, J], BF16, "x_g1")]
         nc.scalar.activation(x_g[0][:], x0_bf[:].indirect(idx[:]), ACT.Copy)
-        turn_x(x_g[0], xt01[:].bitcast(F32)[:, 0 : J // 2], "xt_ps0")
         x1_bf = tile([P, T], BF16, "sq")
         for c in range(0, T, T // 2):
             nc.scalar.copy(x1_bf[:, c : c + T // 2], x_raw[1][:, c : c + T // 2])
         nc.scalar.activation(x_g[1][:], x1_bf[:].indirect(idx[:]), ACT.Copy)
+        xt01 = tile([P, 2 * J], BF16, "x_raw1")
+        turn_x(x_g[0], xt01[:].bitcast(F32)[:, 0 : J // 2], "xt_ps0")
         turn_x(x_g[1], xt01[:].bitcast(F32)[:, J // 2 : J], "xt_ps1")
-        x_g.append(tile([P, J], BF16, "x0_half1"))
-        nc.vector.tensor_copy(x_g[2][:], x_raw[2][:].indirect(idx[:]))
-        turn_x(x_g[2], xt2[:].bitcast(F32), "xt_ps0")
-        gt_bf = tile([P, R, 4], BF16, "x_raw2")
+        xt23 = tile([P, 2 * J], BF16, "sq")
+        for g, reuse, bank in ((2, "x0_half1", "xt_ps2"), (3, "nu1", "c0_ps")):
+            x_g.append(tile([P, J], BF16, reuse))
+            nc.vector.tensor_copy(x_g[g][:], x_raw[g][:].indirect(idx[:]))
+            turn_x(x_g[g], xt23[:].bitcast(F32)[:, (g - 2) * J // 2 : (g - 1) * J // 2], bank)
+        gt_bf = tile([P, R, 4], BF16, "x_raw3")
         nc.vector.tensor_tensor(gt_bf[:], da_ps[:].rearrange("p t r -> p r t"),
                                 js_col[:].unsqueeze(1).to_broadcast([P, R, 4]), ALU.mult)
-        x_g.append(tile([P, J], BF16, "nu1"))
-        nc.vector.tensor_copy(x_g[3][:], x_raw[3][:].indirect(idx[:]))
-        turn_x(x_g[3], xt3[:].bitcast(F32), "c0_ps")
-        gt_q = quantize(gt_bf[:].rearrange("p r t -> p (r t)"), R, "gt", "x_raw3")
-        xq01 = quantize(xt01[:], 2 * P, "xq01", "x_raw2")
-        xq2 = quantize(xt2[:], P, "xq2", "xt01")
-        xq3 = quantize(xt3[:], P, "xq3")
+        xq01 = quantize(xt01[:], 2 * P, "xq01", "js_col")
+        gt_q = quantize(gt_bf[:].rearrange("p r t -> p (r t)"), R, "gt")
+        xq23 = quantize(xt23[:], 2 * P, "xq23")
         res = tile([P, 4, R], F32, "res")
         out_rows = out.rearrange("(p g) r -> p g r", g=4)
-        gw_a = ps.tile([P, 3, R], F32, name="gw_a")
-        gt_op = (gt_q[0][:], gt_q[1][:])
-        for g in range(2):
-            product(gw_a[:, g, :], (xq01[0][:, g * P : (g + 1) * P], xq01[1][:, g * P : (g + 1) * P]), gt_op)
-        product(gw_a[:, 2, :], (xq2[0][:], xq2[1][:]), gt_op)
-        gw_b = ps.tile([P, half], F32, name="a_ps1")
-        product(gw_b[:, 0:R], (xq3[0][:], xq3[1][:]), gt_op)
-        nc.vector.tensor_tensor(res[:, 0:3, :], gw_a[:], old_sb[:, 0:3, :], ALU.add)
-        nc.sync.dma_start(out_rows[:, 0:3, :], res[:, 0:3, :])
-        nc.vector.tensor_tensor(res[:, 3, :], gw_b[:, 0:R], old_sb[:, 3, :], ALU.add)
-        nc.scalar.dma_start(out_rows[:, 3, :], res[:, 3, :])
+        for pair, (xq, bank, queue) in enumerate(((xq01, "gw_a", nc.sync), (xq23, "a_ps1", nc.scalar))):
+            gw = ps.tile([P, 2, R], F32, name=bank)
+            for g in range(2):
+                product(gw[:, g, :], (xq[0][:, g * P : (g + 1) * P], xq[1][:, g * P : (g + 1) * P]), (gt_q[0][:], gt_q[1][:]))
+            rows = slice(2 * pair, 2 * pair + 2)
+            nc.vector.tensor_tensor(res[:, rows, :], gw[:], old_sb[:, rows, :], ALU.add)
+            queue.dma_start(out_rows[:, rows, :], res[:, rows, :])

from contextlib import ExitStack

import concourse.mybir as mybir
from concourse.masks import make_identity

K, R, F, T, J, M = 512, 128, 512, 2048, 512, 256
P = 128
FLOPS = 2 * (K * R * J + F * R * M + J * K * R)

F32 = mybir.dt.float32
BF16 = mybir.dt.bfloat16
I32 = mybir.dt.int32
U32 = mybir.dt.uint32
U16 = mybir.dt.uint16
U8 = mybir.dt.uint8
FP8X4 = mybir.dt.float8_e4m3fn_x4
ALU = mybir.AluOpType
ACT = mybir.ActivationFunctionType


def tile_attend_cpairnear_w_kernel(tc, tab_words, tab_scales, w1, sharp, wo, dy, js, xrows, old, offs, offs2, offs3, out):
    nc = tc.nc
    with ExitStack() as ctx:
        lists = ctx.enter_context(tc.tile_pool(name="lists", bufs=1))
        sb = ctx.enter_context(tc.tile_pool(name="sb", bufs=1))
        ps = ctx.enter_context(tc.psum_pool(name="ps", bufs=1))

        def tile(shape, dtype, name):
            return sb.tile(shape, dtype, name=name, align_bytes=64)

        def quantize(grouped, words, name, reuse=None):
            codes = tile([P, words], U32, reuse or name + "_codes")
            scales = tile([P, words], U8, name + "_scales")
            nc.vector.quantize_mx(out=codes[:].bitcast(FP8X4), scales=scales[:], in_=grouped)
            return codes, scales

        def interleave(grouped, raw):
            nc.scalar.activation(grouped[:].rearrange("p (c i) t -> p c t i", i=4), raw[:].rearrange("p t (c i) -> p c t i", i=4), ACT.Copy)

        def product(acc, lhs, rhs):
            nc.tensor.matmul_mx(out=acc, lhsT=lhs[0].bitcast(FP8X4), lhsT_scale=lhs[1],
                                rhs=rhs[0].bitcast(FP8X4), rhs_scale=rhs[1], start=True, stop=True)

        idx = lists.tile([P, J // 16], U16, name="idx")
        idx2 = lists.tile([P, M // 16], U16, name="idx2")
        idx3 = lists.tile([P, M // 16], U16, name="idx3")
        tab_b = tile([P, T], U8, "tab_b")
        tab_w = tile([P, T], U32, "tab_w")
        nc.vector.memset(tab_b[:].bitcast(I32), 0)
        stage_b = tile([P, T // 4], I32, "stage_b")
        for q in range(4):
            (nc.sync, nc.scalar)[q % 2].dma_start(stage_b[32 * q : 32 * q + 4, :], tab_scales[0, 4 * q : 4 * q + 4, :].bitcast(I32))
        nc.sync.dma_start(idx[:], offs)
        w1_raw = tile([P, 4, R], F32, "w1_raw")
        nc.scalar.dma_start(w1_raw[:], w1.rearrange("(p t) r -> p t r", t=4))
        nc.sync.dma_start(tab_w[:].bitcast(I32), tab_words[0].rearrange("p n t -> p (n t)").bitcast(I32))
        wo_raw = tile([P, 4, R], F32, "wo_raw")
        nc.sync.dma_start(wo_raw[:], wo.rearrange("(p t) r -> p t r", t=4))
        nc.sync.dma_start(idx2[:], offs2)
        nc.sync.dma_start(idx3[:], offs3)
        sharp_col = tile([P, 2], F32, "sharp_col")
        nc.sync.dma_start(sharp_col[:], sharp.rearrange("o (p e) -> p (o e)", e=2))
        dy_raw = tile([P, 4, M], F32, "dy_raw")
        nc.sync.dma_start(dy_raw[:], dy.rearrange("(p t) m -> p t m", t=4))
        x_rows = xrows.rearrange("(p g) t -> g p t", g=4)
        x0_halves = [tile([P, T // 2], F32, "x0_half%d" % h) for h in range(2)]
        x_raw = [None] + [tile([P, T], F32, "x_raw%d" % g) for g in range(1, 4)]
        for h in range(2):
            nc.sync.dma_start(x0_halves[h][:], x_rows[0][:, h * T // 2 : (h + 1) * T // 2])
        js_col = tile([P, 4], F32, "js_col")
        old_sb = tile([P, 4, R], F32, "old_sb")
        for g in range(1, 4):
            if g == 2:
                nc.sync.dma_start(js_col[:], js.rearrange("o (p t) -> p (o t)", t=4))
            nc.sync.dma_start(x_raw[g][:], x_rows[g])
        nc.sync.dma_start(old_sb[:], old.rearrange("(p g) r -> p g r", g=4))

        ident = tile([P, P], F32, "ident")
        make_identity(nc, ident[:])
        s1 = tile([P, J], F32, "s1")
        s2 = tile([P, J], F32, "s2")
        nc.vector.memset(s1[:], 0.0)
        nc.vector.memset(s2[:], 0.0)

        for q in range(4):
            nc.vector.tensor_copy(tab_b[32 * q : 32 * q + 4, :].bitcast(I32), stage_b[32 * q : 32 * q + 4, :])
        w1_bf = tile([P, R, 4], BF16, "w1_bf")
        interleave(w1_bf, w1_raw)
        w1_q = quantize(w1_bf[:].rearrange("p r t -> p (r t)"), R, "w1")
        g_b = tile([P, J], U8, "g_b")
        nc.vector.tensor_copy(g_b[:], tab_b[:].indirect(idx[:]))
        g_w = tile([P, J], U32, "g_w")
        a = tile([P, J], F32, "a")
        half = J // 2
        for h in range(2):
            cols = slice(h * half, (h + 1) * half)
            nc.vector.tensor_copy(g_w[:, cols], tab_w[:].indirect(idx[:, h * half // 16 : (h + 1) * half // 16]))
        a_ps = [ps.tile([P, half], F32, name="a_ps%d" % h) for h in range(2)]
        for h in range(2):
            cols = slice(h * half, (h + 1) * half)
            product(a_ps[h][:], (w1_q[0][:], w1_q[1][:]), (g_w[:, cols], g_b[:, cols]))
        wo_bf = tile([P, R, 4], BF16, "wo_bf")
        interleave(wo_bf, wo_raw)
        dy_bf = tile([P, M, 4], BF16, "dy_bf")
        interleave(dy_bf, dy_raw)
        nc.vector.tensor_copy(a[:, 0:half], a_ps[0][:])
        nc.vector.tensor_copy(a[:, half:J], a_ps[1][:])
        wo_q = quantize(wo_bf[:].rearrange("p r t -> p (r t)"), R, "wo", "tab_w")

        sharp_ps = ps.tile([P, 2, P], F32, name="a_ps0")
        for e in range(2):
            nc.tensor.transpose(sharp_ps[:, e, :], sharp_col[:, e : e + 1].to_broadcast([P, P]), ident[:])

        def turn_x(x_g, xt_words, bank):
            words = x_g[:].bitcast(F32)
            xt_ps = ps.tile([P, 2, P], F32, name=bank)
            for u in range(2):
                nc.tensor.transpose(xt_ps[:, u, :], words[:, u : J // 2 : 2], ident[:])
            nc.scalar.copy(xt_words.rearrange("p (k u) -> p k u", u=2), xt_ps[:].rearrange("p u k -> p k u"))

        x0_bf = tile([P, T], BF16, "x0_bf")
        for h in range(2):
            nc.scalar.copy(x0_bf[:, h * T // 2 : (h + 1) * T // 2], x0_halves[h][:])
        parts = [slice(0, M // 2), slice(M // 2, M)]
        offsets = [slice(0, M // 32), slice(M // 32, M // 16)]
        a3 = tile([P, M], F32, "wo_raw")
        ds = tile([P, M], F32, "ds")
        sq = tile([P, M], F32, "sq")
        u1 = tile([P, M], F32, "x0_half1")
        coef = tile([P, M], F32, "coef")
        nu1 = tile([P, M], F32, "nu1")
        for h in range(2):
            nc.vector.tensor_copy(a3[:, parts[h]], a[:].indirect(idx3[:, offsets[h]]))
        dy_q = quantize(dy_bf[:].rearrange("p m t -> p (m t)"), M, "dy")
        c0_ps = ps.tile([P, M], F32, name="c0_ps")
        product(c0_ps[:], (wo_q[0][:], wo_q[1][:]), (dy_q[0][:], dy_q[1][:]))
        dl = tile([P, M], F32, "dy_raw")
        for h in range(2):
            nc.vector.tensor_tensor(dl[:, parts[h]], a[:].indirect(idx2[:, offsets[h]]), a3[:, parts[h]], ALU.subtract)
        for h in range(2):
            nc.vector.tensor_tensor(ds[:, parts[h]].rearrange("p (n e) -> p n e", e=2), dl[:, parts[h]].rearrange("p (n e) -> p n e", e=2),
                                    sharp_ps[:, :, 64 * h : 64 * h + 64].rearrange("p e n -> p n e"), ALU.mult)
        for h in range(2):
            nc.vector.tensor_tensor(sq[:, parts[h]], ds[:, parts[h]], dl[:, parts[h]], ALU.mult)
            nc.scalar.activation(u1[:, parts[h]], sq[:, parts[h]], ACT.Exp, scale=-1.0)
            nc.vector.scalar_tensor_tensor(coef[:, parts[h]], ds[:, parts[h]], -2.0, c0_ps[:, parts[h]], ALU.mult, ALU.mult)
        for h in range(2):
            nc.scalar.activation(nu1[:, parts[h]], u1[:, parts[h]], ACT.Copy, scale=-1.0)
        for h in range(2):
            nc.vector.tensor_tensor(s1[:].indirect(idx2[:, offsets[h]]), coef[:, parts[h]], u1[:, parts[h]], ALU.mult)
            nc.vector.tensor_tensor(s2[:].indirect(idx3[:, offsets[h]]), coef[:, parts[h]], nu1[:, parts[h]], ALU.mult)

        da_ps = ps.tile([P, 4, R], F32, name="da_ps")
        for i, s in enumerate((s1, s2)):
            for t in range(4):
                nc.tensor.matmul(da_ps[:, t, :], s[:, t:J:4], ident[:], is_transpose=True,
                                 start=(i == 0 and t == 0), stop=(i == 1 and t == 3))

        x_g = [tile([P, J], BF16, "x_g0"), tile([P, J], BF16, "x_g1")]
        nc.scalar.activation(x_g[0][:], x0_bf[:].indirect(idx[:]), ACT.Copy)
        x1_bf = tile([P, T], BF16, "sq")
        for c in range(0, T, T // 2):
            nc.scalar.copy(x1_bf[:, c : c + T // 2], x_raw[1][:, c : c + T // 2])
        nc.scalar.activation(x_g[1][:], x1_bf[:].indirect(idx[:]), ACT.Copy)
        xt01 = tile([P, 2 * J], BF16, "x_raw1")
        turn_x(x_g[0], xt01[:].bitcast(F32)[:, 0 : J // 2], "xt_ps0")
        turn_x(x_g[1], xt01[:].bitcast(F32)[:, J // 2 : J], "xt_ps1")
        xt23 = tile([P, 2 * J], BF16, "sq")
        for g, reuse, bank in ((2, "x0_half1", "xt_ps2"), (3, "nu1", "c0_ps")):
            x_g.append(tile([P, J], BF16, reuse))
            nc.vector.tensor_copy(x_g[g][:], x_raw[g][:].indirect(idx[:]))
            turn_x(x_g[g], xt23[:].bitcast(F32)[:, (g - 2) * J // 2 : (g - 1) * J // 2], bank)
        gt_bf = tile([P, R, 4], BF16, "x_raw3")
        nc.vector.tensor_tensor(gt_bf[:], da_ps[:].rearrange("p t r -> p r t"),
                                js_col[:].unsqueeze(1).to_broadcast([P, R, 4]), ALU.mult)
        xq01 = quantize(xt01[:], 2 * P, "xq01", "js_col")
        gt_q = quantize(gt_bf[:].rearrange("p r t -> p (r t)"), R, "gt")
        xq23 = quantize(xt23[:], 2 * P, "xq23")
        res = tile([P, 4, R], F32, "res")
        out_rows = out.rearrange("(p g) r -> p g r", g=4)
        for pair, (xq, bank, queue) in enumerate(((xq01, "gw_a", nc.sync), (xq23, "a_ps1", nc.scalar))):
            gw = ps.tile([P, 2, R], F32, name=bank)
            for g in range(2):
                product(gw[:, g, :], (xq[0][:, g * P : (g + 1) * P], xq[1][:, g * P : (g + 1) * P]), (gt_q[0][:], gt_q[1][:]))
            rows = slice(2 * pair, 2 * pair + 2)
            nc.vector.tensor_tensor(res[:, rows, :], gw[:], old_sb[:, rows, :], ALU.add)
            queue.dma_start(out_rows[:, rows, :], res[:, rows, :])
